import numpy as np, ml_dtypes
CORES = [120,124,248,252,376,380,504,508]
N = 8
import mx_ref
NC, HD, G = 256, 1, 4
C, DEC = np.float32(0.043), np.float32(0.85)
BF = ml_dtypes.bfloat16
def cut(t, i, w=512):
    return t[:, w * i:w * i + w]
def tile(rs):
    return np.stack(rs, axis=2).reshape(128, -1).astype(BF)
def layer(w, X):
    out = []
    for i in range(G):
        for t in range(len(X)):
            p = mx_ref.matmul(mx_ref.quantize(cut(w, len(X) * i + t)), X[t])
            z = p if t == 0 else z + p
        out.append(z)
    return out
def pick(b):
    s = np.zeros((128, 128, 4), np.float32)
    s[np.arange(128), np.arange(128), b] = 1.0
    return mx_ref.quantize(s.reshape(128, 512).astype(BF))
def setup_inputs(rng):
    def f(*shape):
        return mx_ref.flush((rng.standard_normal(shape, dtype=np.float32) * np.exp2(rng.integers(-2, 3, shape[:-1] + (1,)))).astype(BF))
    return {"k": f(N, 128, HD * 4 * 512), "v": f(N, 128, HD * 512), "q": f(N, 128, HD * 4 * NC)}
def setup_inputs_blocks(rng):
    d = setup_inputs(rng)
    for k in ("k", "v", "q"): d[k] = mx_ref.spread(d[k], rng, 4)
    return d
def setup_inputs_wide(rng):
    d = setup_inputs(rng)
    for k in ("k", "v", "q"): d[k] = mx_ref.flush((d[k].astype(np.float32) * np.exp2(rng.integers(-4, 5, (N, 1, 1))).astype(np.float32)).astype(BF))
    return d
def setup_inputs_zeros(rng):
    d = setup_inputs(rng); v = d["v"].reshape(N, 128, -1, 4).copy()
    v[np.broadcast_to((rng.random((N, 1, v.shape[2], 1)) < 0.33), v.shape)] = 0
    d["v"] = v.reshape(d["v"].shape)
    return d
def reference(k, v, q):
    S = [pick(t) for t in range(4)]
    y = np.zeros((N, 128, HD * NC), np.float32)
    for a in range(HD):
        for r in range(N):
            R = [z * C for z in layer(cut(k[r], a, 4 * 512), [mx_ref.quantize(cut(v[r], a))])]
            if r > 0: R = [R[t] + mx_ref.matmul(S[t], s) * DEC for t in range(4)]
            s = mx_ref.quantize(tile(R))
            y[r][:, NC * a:NC * a + NC] = mx_ref.matmul(s, mx_ref.quantize(cut(q[r], a, 4 * NC)))
    return {"y": y}

@@ -1,0 +1,141 @@
+import numpy as np
+from concourse.bass import DstId, RemoteDMATransfer
+from concourse.mybir import dt, AluOpType, AxisListType, ActivationFunctionType
+
+P, W = 128, 128
+C = float(np.float32(0.043))
+DEC = float(np.float32(0.85))
+BANK = 512
+
+SCRATCH = {
+    "vb": ("sbuf", [P, 512], "bfloat16"), "kb": ("sbuf", [P, 2048], "bfloat16"), "qb": ("sbuf", [P, 1024], "bfloat16"),
+    "vc": ("sbuf", [P, 128], "float8_e4m3fn_x4"), "vs": ("sbuf", [P, 128], "uint8"),
+    "kc": ("sbuf", [P, 512], "float8_e4m3fn_x4"), "ks": ("sbuf", [P, 512], "uint8"),
+    "qc": ("sbuf", [P, 256], "float8_e4m3fn_x4"), "qs": ("sbuf", [P, 256], "uint8"),
+    "ones": ("sbuf", [P, 128], "bfloat16"), "eye": ("sbuf", [P, 128], "bfloat16"),
+    "pb": ("sbuf", [P, 2048], "bfloat16"),
+    "pc": ("sbuf", [P, 512], "float8_e4m3fn_x4"), "ps": ("sbuf", [P, 512], "uint8"),
+    "ic": ("sbuf", [P, W], "float8_e4m3fn_x4"), "isc": ("sbuf", [P, W], "uint8"),
+    "hb": ("sbuf", [P, 4 * W], "bfloat16"),
+    "hc": ("sbuf", [P, W], "float8_e4m3fn_x4"), "hs": ("sbuf", [P, W], "uint8"),
+    "zc": ("sbuf", [P, 4 * W], "float32"), "dd": ("sbuf", [P, 4 * W], "float32"),
+    "yb": ("sbuf", [P, 256], "float32"),
+    "z": ("psum", [P, 4 * BANK], "float32"), "d": ("psum", [P, 4 * BANK], "float32"),
+}
+SEMAPHORES = (["lv", "lk0", "lk1", "lq", "one", "zero", "eyed", "picked", "qv", "qp", "qq", "zs", "hw", "ha", "hq",
+               "arr", "sent", "y0", "y1", "yc0", "yc1", "st"]
+              + ["qk%d" % i for i in range(4)] + ["zz%d" % i for i in range(4)]
+              + ["dm%d" % i for i in range(4)] + ["dx%d" % i for i in range(4)])
+
+
+def engines(topo, src, dst):
+    allowed = topo.mask(src, dst)
+    bits = [e for e in range(16) if (allowed >> e) & 1]
+    use = bits[::max(1, len(bits) // 8)]
+    return sum(1 << e for e in use), len(use)
+
+
+def bank(t, b, n=W):
+    return t[:, BANK * b:BANK * b + n]
+
+
+def rank_program(g, core, T, topo):
+    r = T.rank_of(core)
+    if r is None:
+        return
+    cores = list(T.cores)
+    first, last = r == 0, r == len(cores) - 1
+    sem = T.sem
+    V, S, PE, SY = g.vector, g.scalar, g.tensor, g.sync
+    copy, mult, add = ActivationFunctionType.Copy, AluOpType.mult, AluOpType.add
+    cols = lambda b: slice(W * b, W * b + W)
+    sent_n = 0 if last else 2 * engines(topo, core, cores[r + 1])[1]
+    arr_n = 0 if first else 2 * engines(topo, cores[r - 1], core)[1]
+
+    SY.dma_start(T.vb[:], T.v[:]).then_inc(sem.lv, 16)
+    S.dma_start(T.kb[:, 0:1024], T.k[:, 0:1024]).then_inc(sem.lk0, 16)
+    SY.dma_start(T.kb[:, 1024:2048], T.k[:, 1024:2048]).then_inc(sem.lk1, 16)
+    if first:
+        SY.wait_ge(sem.sent, sent_n)
+    SY.dma_start(T.qb[:], T.q[:]).then_inc(sem.lq, 16)
+
+    if not first:
+        V.memset(T.ones[:], 1.0).then_inc(sem.one, 1)
+        V.memset(T.pb[:], 0.0).then_inc(sem.zero, 1)
+        g.wait_ge(sem.one, 1)
+        g.affine_select(T.eye[:], T.ones[:], [[-1, 128]], AluOpType.is_equal, 0.0, 0, 1).then_inc(sem.eyed, 1)
+        S.wait_ge(sem.zero, 1)
+        S.wait_ge(sem.eyed, 1)
+        for b in range(4):
+            S.activation(T.pb[:, 512 * b + b:512 * b + 512:4], T.eye[:], copy).then_inc(sem.picked, 1)
+
+    V.wait_ge(sem.lv, 16)
+    V.quantize_mx(T.vc[:], T.vs[:], T.vb[:]).then_inc(sem.qv, 1)
+    for b in range(4):
+        if b % 2 == 0:
+            V.wait_ge(sem["lk%d" % (b // 2)], 16)
+        V.quantize_mx(T.kc[:, cols(b)], T.ks[:, cols(b)], T.kb[:, 512 * b:512 * b + 512]).then_inc(sem["qk%d" % b], 1)
+    PE.wait_ge(sem.qv, 1)
+    for b in range(4):
+        PE.wait_ge(sem["qk%d" % b], 1)
+        PE.matmul_mx(bank(T.z, b), T.kc[:, cols(b)], T.ks[:, cols(b)], T.vc[:], T.vs[:], True, True).then_inc(sem["zz%d" % b], 1)
+
+    def quantise_q():
+        V.wait_ge(sem.lq, 16)
+        V.quantize_mx(T.qc[:], T.qs[:], T.qb[:]).then_inc(sem.qq, 1)
+
+    if first:
+        for b in range(3):
+            S.wait_ge(sem["zz%d" % b], 1)
+            S.activation(T.hb[:, b:4 * W:4], bank(T.z, b), copy, scale=C).then_inc(sem.ha, 1)
+        V.wait_ge(sem.zz3, 1)
+        V.tensor_scalar(T.hb[:, 3:4 * W:4], bank(T.z, 3), C, None, mult).then_inc(sem.hw, 1)
+        V.wait_ge(sem.ha, 3)
+        V.wait_ge(sem.hw, 1)
+    else:
+        for b in range(4):
+            S.wait_ge(sem["zz%d" % b], 1)
+            S.activation(T.zc[:, cols(b)], bank(T.z, b), copy, scale=C).then_inc(sem.zs, 1)
+        V.wait_ge(sem.picked, 4)
+        V.quantize_mx(T.pc[:], T.ps[:], T.pb[:]).then_inc(sem.qp, 1)
+        quantise_q()
+        V.wait_ge(sem.zs, 4)
+        PE.wait_ge(sem.qp, 1)
+        PE.wait_ge(sem.arr, arr_n)
+        for b in range(4):
+            PE.matmul_mx(bank(T.d, b), T.pc[:, cols(b)], T.ps[:, cols(b)], T.ic[:], T.isc[:], True, True).then_inc(sem["dm%d" % b], 1)
+        V.wait_ge(sem.dm0, 1)
+        V.tensor_scalar(T.dd[:, cols(0)], bank(T.d, 0), DEC, None, mult).then_inc(sem.dx0, 1)
+        for b in range(1, 4):
+            S.wait_ge(sem["dm%d" % b], 1)
+            S.activation(T.dd[:, cols(b)], bank(T.d, b), copy, scale=DEC).then_inc(sem["dx%d" % b], 1)
+        for b in range(4):
+            V.wait_ge(sem["dx%d" % b], 1)
+            V.tensor_tensor(T.hb[:, b:4 * W:4], T.dd[:, cols(b)], T.zc[:, cols(b)], add).then_inc(sem.hw, 1)
+        V.wait_ge(sem.hw, 4)
+    V.quantize_mx(T.hc[:], T.hs[:], T.hb[:]).then_inc(sem.hq, 1)
+
+    if not last:
+        nxt = cores[r + 1]
+        mask, _ = engines(topo, core, nxt)
+        rid, pid = topo.addr(nxt, core)
+        g.wait_ge(sem.hq, 1)
+        g.remote_dma(T.ic[:].bitcast(dt.uint8), T.hc[:].bitcast(dt.uint8), sem.arr, sem.sent, pid, rid, mask)
+        g.remote_dma(T.isc[:], T.hs[:], sem.arr, sem.sent, pid, rid, mask)
+
+    if first:
+        quantise_q()
+    PE.wait_ge(sem.hq, 1)
+    PE.wait_ge(sem.qq, 1)
+    for i in range(2):
+        PE.matmul_mx(bank(T.z, i), T.hc[:], T.hs[:], T.qc[:, cols(i)], T.qs[:, cols(i)], True, True).then_inc(sem["y%d" % i], 1)
+    S.wait_ge(sem.y0, 1)
+    S.activation(T.yb[:, cols(0)], bank(T.z, 0), copy).then_inc(sem.yc0, 1)
+    V.wait_ge(sem.y1, 1)
+    V.tensor_copy(T.yb[:, cols(1)], bank(T.z, 1)).then_inc(sem.yc1, 1)
+    for q, i in ((S, 0), (SY, 1)):
+        if not last:
+            q.wait_ge(sem.sent, sent_n)
+        q.wait_ge(sem["yc%d" % i], 1)
+        q.dma_start(T.y[:, cols(i)], T.yb[:, cols(i)]).then_inc(sem.st, 16)
+    SY.wait_ge(sem.st, 32)

@@ -6,6 +6,7 @@ P, W = 128, 128
 C = float(np.float32(0.043))
 DEC = float(np.float32(0.85))
 BANK = 512
+SHARE = 32
 
 SCRATCH = {
     "vb": ("sbuf", [P, 512], "bfloat16"), "kb": ("sbuf", [P, 2048], "bfloat16"), "qb": ("sbuf", [P, 1024], "bfloat16"),
@@ -23,16 +24,24 @@ SCRATCH = {
     "z": ("psum", [P, 4 * BANK], "float32"), "d": ("psum", [P, 4 * BANK], "float32"),
 }
 SEMAPHORES = (["lv", "lk0", "lk1", "lq", "one", "zero", "eyed", "picked", "qv", "qp", "qq", "zs", "hw", "ha", "hq",
-               "arr", "sent", "y0", "y1", "yc0", "yc1", "st"]
+               "arr", "sent", "parr", "psent", "y0", "y1", "yc0", "yc1", "st"]
               + ["qk%d" % i for i in range(4)] + ["zz%d" % i for i in range(4)]
               + ["dm%d" % i for i in range(4)] + ["dx%d" % i for i in range(4)])
 
 
 def engines(topo, src, dst):
-    allowed = topo.mask(src, dst)
-    bits = [e for e in range(16) if (allowed >> e) & 1]
-    use = bits[::max(1, len(bits) // 8)]
-    return sum(1 << e for e in use), len(use)
+    mask = topo.mask(src, dst)
+    return mask, bin(mask).count("1")
+
+
+def made(r):
+    if r == 0:
+        return 0, W
+    return (0, 4 * W - SHARE) if r % 2 == 0 else (SHARE, 4 * W)
+
+
+def given(r):
+    return (0, SHARE) if r % 2 == 0 else (4 * W - SHARE, 4 * W)
 
 
 def bank(t, b, n=W):
@@ -59,15 +68,29 @@ def rank_program(g, core, T, topo):
         SY.wait_ge(sem.sent, sent_n)
     SY.dma_start(T.qb[:], T.q[:]).then_inc(sem.lq, 16)
 
-    if not first:
-        V.memset(T.ones[:], 1.0).then_inc(sem.one, 1)
-        V.memset(T.pb[:], 0.0).then_inc(sem.zero, 1)
-        g.wait_ge(sem.one, 1)
-        g.affine_select(T.eye[:], T.ones[:], [[-1, 128]], AluOpType.is_equal, 0.0, 0, 1).then_inc(sem.eyed, 1)
-        S.wait_ge(sem.zero, 1)
-        S.wait_ge(sem.eyed, 1)
-        for b in range(4):
-            S.activation(T.pb[:, 512 * b + b:512 * b + 512:4], T.eye[:], copy).then_inc(sem.picked, 1)
+    lo, hi = made(r)
+    V.memset(T.ones[:], 1.0).then_inc(sem.one, 1)
+    V.memset(T.pb[:, 4 * lo:4 * hi], 0.0).then_inc(sem.zero, 1)
+    g.wait_ge(sem.one, 1)
+    g.affine_select(T.eye[:], T.ones[:], [[-1, 128]], AluOpType.is_equal, 0.0, 0, 1).then_inc(sem.eyed, 1)
+    S.wait_ge(sem.zero, 1)
+    S.wait_ge(sem.eyed, 1)
+    parts = 0
+    for b in range(4):
+        j0, j1 = max(0, lo - W * b), min(W, hi - W * b)
+        if j0 < j1:
+            S.activation(T.pb[:, 512 * b + 4 * j0 + b:512 * b + 4 * j1:4], T.eye[:, j0:j1], copy).then_inc(sem.picked, 1)
+            parts += 1
+    V.wait_ge(sem.picked, parts)
+    V.quantize_mx(T.pc[:, lo:hi], T.ps[:, lo:hi], T.pb[:, 4 * lo:4 * hi]).then_inc(sem.qp, 1)
+    if not last:
+        nxt = cores[r + 1]
+        mask, _ = engines(topo, core, nxt)
+        rid, pid = topo.addr(nxt, core)
+        s0, s1 = given(r)
+        g.wait_ge(sem.qp, 1)
+        g.remote_dma(T.pc[:, s0:s1].bitcast(dt.uint8), T.pc[:, s0:s1].bitcast(dt.uint8), sem.parr, sem.psent, pid, rid, mask)
+        g.remote_dma(T.ps[:, s0:s1], T.ps[:, s0:s1], sem.parr, sem.psent, pid, rid, mask)
 
     V.wait_ge(sem.lv, 16)
     V.quantize_mx(T.vc[:], T.vs[:], T.vb[:]).then_inc(sem.qv, 1)
@@ -96,11 +119,10 @@ def rank_program(g, core, T, topo):
         for b in range(4):
             S.wait_ge(sem["zz%d" % b], 1)
             S.activation(T.zc[:, cols(b)], bank(T.z, b), copy, scale=C).then_inc(sem.zs, 1)
-        V.wait_ge(sem.picked, 4)
-        V.quantize_mx(T.pc[:], T.ps[:], T.pb[:]).then_inc(sem.qp, 1)
         quantise_q()
         V.wait_ge(sem.zs, 4)
         PE.wait_ge(sem.qp, 1)
+        PE.wait_ge(sem.parr, arr_n)
         PE.wait_ge(sem.arr, arr_n)
         for b in range(4):
             PE.matmul_mx(bank(T.d, b), T.pc[:, cols(b)], T.ps[:, cols(b)], T.ic[:], T.isc[:], True, True).then_inc(sem["dm%d" % b], 1)
@@ -116,9 +138,6 @@ def rank_program(g, core, T, topo):
     V.quantize_mx(T.hc[:], T.hs[:], T.hb[:]).then_inc(sem.hq, 1)
 
     if not last:
-        nxt = cores[r + 1]
-        mask, _ = engines(topo, core, nxt)
-        rid, pid = topo.addr(nxt, core)
         g.wait_ge(sem.hq, 1)
         g.remote_dma(T.ic[:].bitcast(dt.uint8), T.hc[:].bitcast(dt.uint8), sem.arr, sem.sent, pid, rid, mask)
         g.remote_dma(T.isc[:], T.hs[:], sem.arr, sem.sent, pid, rid, mask)
@@ -138,4 +157,6 @@ def rank_program(g, core, T, topo):
             q.wait_ge(sem.sent, sent_n)
         q.wait_ge(sem["yc%d" % i], 1)
         q.dma_start(T.y[:, cols(i)], T.yb[:, cols(i)]).then_inc(sem.st, 16)
+    if not last:
+        SY.wait_ge(sem.psent, sent_n)
     SY.wait_ge(sem.st, 32)

import numpy as np
from concourse.bass import DstId, RemoteDMATransfer
from concourse.mybir import dt, AluOpType, AxisListType, ActivationFunctionType

P, W = 128, 128
C = float(np.float32(0.043))
DEC = float(np.float32(0.85))
BANK = 512
SHARE = 32

SCRATCH = {
    "vb": ("sbuf", [P, 512], "bfloat16"), "kb": ("sbuf", [P, 2048], "bfloat16"), "qb": ("sbuf", [P, 1024], "bfloat16"),
    "vc": ("sbuf", [P, 128], "float8_e4m3fn_x4"), "vs": ("sbuf", [P, 128], "uint8"),
    "kc": ("sbuf", [P, 512], "float8_e4m3fn_x4"), "ks": ("sbuf", [P, 512], "uint8"),
    "qc": ("sbuf", [P, 256], "float8_e4m3fn_x4"), "qs": ("sbuf", [P, 256], "uint8"),
    "ones": ("sbuf", [P, 128], "bfloat16"), "eye": ("sbuf", [P, 128], "bfloat16"),
    "pb": ("sbuf", [P, 2048], "bfloat16"),
    "pc": ("sbuf", [P, 512], "float8_e4m3fn_x4"), "ps": ("sbuf", [P, 512], "uint8"),
    "ic": ("sbuf", [P, W], "float8_e4m3fn_x4"), "isc": ("sbuf", [P, W], "uint8"),
    "hb": ("sbuf", [P, 4 * W], "bfloat16"),
    "hc": ("sbuf", [P, W], "float8_e4m3fn_x4"), "hs": ("sbuf", [P, W], "uint8"),
    "zc": ("sbuf", [P, 4 * W], "float32"), "dd": ("sbuf", [P, 4 * W], "float32"),
    "yb": ("sbuf", [P, 256], "float32"),
    "z": ("psum", [P, 4 * BANK], "float32"), "d": ("psum", [P, 4 * BANK], "float32"),
}
SEMAPHORES = (["lv", "lk0", "lk1", "lq", "one", "zero", "eyed", "picked", "qv", "qp", "qq", "zs", "hw", "ha", "hq",
               "arr", "sent", "parr", "psent", "y0", "y1", "yc0", "yc1", "st"]
              + ["qk%d" % i for i in range(4)] + ["zz%d" % i for i in range(4)]
              + ["dm%d" % i for i in range(4)] + ["dx%d" % i for i in range(4)])


def engines(topo, src, dst):
    mask = topo.mask(src, dst)
    return mask, bin(mask).count("1")


def made(r):
    if r == 0:
        return 0, W
    return (0, 4 * W - SHARE) if r % 2 == 0 else (SHARE, 4 * W)


def given(r):
    return (0, SHARE) if r % 2 == 0 else (4 * W - SHARE, 4 * W)


def bank(t, b, n=W):
    return t[:, BANK * b:BANK * b + n]


def rank_program(g, core, T, topo):
    r = T.rank_of(core)
    if r is None:
        return
    cores = list(T.cores)
    first, last = r == 0, r == len(cores) - 1
    sem = T.sem
    V, S, PE, SY = g.vector, g.scalar, g.tensor, g.sync
    copy, mult, add = ActivationFunctionType.Copy, AluOpType.mult, AluOpType.add
    cols = lambda b: slice(W * b, W * b + W)
    sent_n = 0 if last else 2 * engines(topo, core, cores[r + 1])[1]
    arr_n = 0 if first else 2 * engines(topo, cores[r - 1], core)[1]

    SY.dma_start(T.vb[:], T.v[:]).then_inc(sem.lv, 16)
    S.dma_start(T.kb[:, 0:1024], T.k[:, 0:1024]).then_inc(sem.lk0, 16)
    SY.dma_start(T.kb[:, 1024:2048], T.k[:, 1024:2048]).then_inc(sem.lk1, 16)
    if first:
        SY.wait_ge(sem.sent, sent_n)
    SY.dma_start(T.qb[:], T.q[:]).then_inc(sem.lq, 16)

    lo, hi = made(r)
    V.memset(T.ones[:], 1.0).then_inc(sem.one, 1)
    V.memset(T.pb[:, 4 * lo:4 * hi], 0.0).then_inc(sem.zero, 1)
    g.wait_ge(sem.one, 1)
    g.affine_select(T.eye[:], T.ones[:], [[-1, 128]], AluOpType.is_equal, 0.0, 0, 1).then_inc(sem.eyed, 1)
    S.wait_ge(sem.zero, 1)
    S.wait_ge(sem.eyed, 1)
    parts = 0
    for b in range(4):
        j0, j1 = max(0, lo - W * b), min(W, hi - W * b)
        if j0 < j1:
            S.activation(T.pb[:, 512 * b + 4 * j0 + b:512 * b + 4 * j1:4], T.eye[:, j0:j1], copy).then_inc(sem.picked, 1)
            parts += 1
    V.wait_ge(sem.picked, parts)
    V.quantize_mx(T.pc[:, lo:hi], T.ps[:, lo:hi], T.pb[:, 4 * lo:4 * hi]).then_inc(sem.qp, 1)
    if not last:
        nxt = cores[r + 1]
        mask, _ = engines(topo, core, nxt)
        rid, pid = topo.addr(nxt, core)
        s0, s1 = given(r)
        g.wait_ge(sem.qp, 1)
        g.remote_dma(T.pc[:, s0:s1].bitcast(dt.uint8), T.pc[:, s0:s1].bitcast(dt.uint8), sem.parr, sem.psent, pid, rid, mask)
        g.remote_dma(T.ps[:, s0:s1], T.ps[:, s0:s1], sem.parr, sem.psent, pid, rid, mask)

    V.wait_ge(sem.lv, 16)
    V.quantize_mx(T.vc[:], T.vs[:], T.vb[:]).then_inc(sem.qv, 1)
    for b in range(4):
        if b % 2 == 0:
            V.wait_ge(sem["lk%d" % (b // 2)], 16)
        V.quantize_mx(T.kc[:, cols(b)], T.ks[:, cols(b)], T.kb[:, 512 * b:512 * b + 512]).then_inc(sem["qk%d" % b], 1)
    PE.wait_ge(sem.qv, 1)
    for b in range(4):
        PE.wait_ge(sem["qk%d" % b], 1)
        PE.matmul_mx(bank(T.z, b), T.kc[:, cols(b)], T.ks[:, cols(b)], T.vc[:], T.vs[:], True, True).then_inc(sem["zz%d" % b], 1)

    def quantise_q():
        V.wait_ge(sem.lq, 16)
        V.quantize_mx(T.qc[:], T.qs[:], T.qb[:]).then_inc(sem.qq, 1)

    if first:
        for b in range(3):
            S.wait_ge(sem["zz%d" % b], 1)
            S.activation(T.hb[:, b:4 * W:4], bank(T.z, b), copy, scale=C).then_inc(sem.ha, 1)
        V.wait_ge(sem.zz3, 1)
        V.tensor_scalar(T.hb[:, 3:4 * W:4], bank(T.z, 3), C, None, mult).then_inc(sem.hw, 1)
        V.wait_ge(sem.ha, 3)
        V.wait_ge(sem.hw, 1)
    else:
        for b in range(4):
            S.wait_ge(sem["zz%d" % b], 1)
            S.activation(T.zc[:, cols(b)], bank(T.z, b), copy, scale=C).then_inc(sem.zs, 1)
        quantise_q()
        V.wait_ge(sem.zs, 4)
        PE.wait_ge(sem.qp, 1)
        PE.wait_ge(sem.parr, arr_n)
        PE.wait_ge(sem.arr, arr_n)
        for b in range(4):
            PE.matmul_mx(bank(T.d, b), T.pc[:, cols(b)], T.ps[:, cols(b)], T.ic[:], T.isc[:], True, True).then_inc(sem["dm%d" % b], 1)
        V.wait_ge(sem.dm0, 1)
        V.tensor_scalar(T.dd[:, cols(0)], bank(T.d, 0), DEC, None, mult).then_inc(sem.dx0, 1)
        for b in range(1, 4):
            S.wait_ge(sem["dm%d" % b], 1)
            S.activation(T.dd[:, cols(b)], bank(T.d, b), copy, scale=DEC).then_inc(sem["dx%d" % b], 1)
        for b in range(4):
            V.wait_ge(sem["dx%d" % b], 1)
            V.tensor_tensor(T.hb[:, b:4 * W:4], T.dd[:, cols(b)], T.zc[:, cols(b)], add).then_inc(sem.hw, 1)
        V.wait_ge(sem.hw, 4)
    V.quantize_mx(T.hc[:], T.hs[:], T.hb[:]).then_inc(sem.hq, 1)

    if not last:
        g.wait_ge(sem.hq, 1)
        g.remote_dma(T.ic[:].bitcast(dt.uint8), T.hc[:].bitcast(dt.uint8), sem.arr, sem.sent, pid, rid, mask)
        g.remote_dma(T.isc[:], T.hs[:], sem.arr, sem.sent, pid, rid, mask)

    if first:
        quantise_q()
    PE.wait_ge(sem.hq, 1)
    PE.wait_ge(sem.qq, 1)
    for i in range(2):
        PE.matmul_mx(bank(T.z, i), T.hc[:], T.hs[:], T.qc[:, cols(i)], T.qs[:, cols(i)], True, True).then_inc(sem["y%d" % i], 1)
    S.wait_ge(sem.y0, 1)
    S.activation(T.yb[:, cols(0)], bank(T.z, 0), copy).then_inc(sem.yc0, 1)
    V.wait_ge(sem.y1, 1)
    V.tensor_copy(T.yb[:, cols(1)], bank(T.z, 1)).then_inc(sem.yc1, 1)
    for q, i in ((S, 0), (SY, 1)):
        if not last:
            q.wait_ge(sem.sent, sent_n)
        q.wait_ge(sem["yc%d" % i], 1)
        q.dma_start(T.y[:, cols(i)], T.yb[:, cols(i)]).then_inc(sem.st, 16)
    if not last:
        SY.wait_ge(sem.psent, sent_n)
    SY.wait_ge(sem.st, 32)
